import numpy as np
import ml_dtypes


def mxq(x, axis, fmt="e4m3"):
    dtype, down = {"e4m3": (ml_dtypes.float8_e4m3fn, 7), "e5m2": (ml_dtypes.float8_e5m2, 14)}[fmt]
    v = np.moveaxis(np.asarray(x, np.float32).astype(ml_dtypes.bfloat16).astype(np.float64), axis, -1)
    blocks = v.reshape(v.shape[:-1] + (-1, 32))
    amax = np.abs(blocks).max(-1, keepdims=True)
    byte = np.maximum(np.where(amax > 0, np.frexp(amax)[1] - 1 + 127, 0) - down, 1)
    scale = np.exp2(byte - 127.0)
    codes = (blocks / scale).astype(np.float32).astype(dtype).astype(np.float64)
    return np.moveaxis((codes * scale).reshape(v.shape), -1, axis)


WIDE = False


def mx_kscale(k):
    if not WIDE:
        return np.ones(k)
    levels = np.array([10, -10, 5, -5, 0])
    if k % 512:
        return np.exp2(np.random.permutation(np.resize(levels, k // 32))).repeat(32)
    a = np.empty((k // 512, 16))
    for p in range(k // 512):
        a[p, :8] = np.random.permutation(np.resize(levels, 8))
        for g in range(8):
            far = levels[np.abs(levels - a[p, g]) >= 10]
            a[p, g + 8] = far[np.random.randint(len(far))]
    return np.exp2(a.ravel()).repeat(32)


def f64(x):
    return np.asarray(x).astype(np.float64)


def striped(idx):
    return np.tile(idx.reshape(-1, 16).T, (8, 1)).astype(np.uint16)


def unstriped(offs):
    return offs[:16].T.reshape(-1).astype(np.int64)


def pack_weight(w):
    k, n = w.shape
    w = f64(np.asarray(w, np.float32).astype(ml_dtypes.bfloat16)).reshape(k // 32, 32, n)
    amax = np.abs(w).max(1)
    byte = np.clip(np.where(amax > 0, np.frexp(amax)[1] - 1 + 127 - 7, 1), 1, 254)
    scaled = (w * np.exp2(127.0 - byte)[:, None, :]).reshape(k, n).astype(np.float32)
    words = np.ascontiguousarray(scaled.reshape(k // 512, 128, 4, n).transpose(0, 1, 3, 2)).astype(ml_dtypes.float8_e4m3fn).view(np.uint8)
    return words, np.ascontiguousarray(byte.astype(np.uint8).reshape(k // 512, 16, n))


def unpack_weight(words, scales):
    g, p, n, _ = words.shape
    vals = np.ascontiguousarray(words).view(ml_dtypes.float8_e4m3fn).astype(np.float64) * np.repeat(np.exp2(scales.astype(np.float64) - 127.0), 8, axis=1)[..., None]
    return vals.transpose(0, 1, 3, 2).reshape(g * 512, n)


def relu(v):
    return np.maximum(v, 0.0)


K, T, S, N, H = 512, 2048, 512, 256, 512


def setup_inputs():
    n = np.random.standard_normal
    s = mx_kscale(K)[:, None]
    u = mx_kscale(H)
    packed_xT = pack_weight(n((K, T)) * s)
    return {
        "x_words": packed_xT[0],
        "x_scales": packed_xT[1],
        "w1": (n((K, H)) / np.sqrt(K) / s).astype(np.float32),
        "w2": (n((K, H)) / np.sqrt(K) / s).astype(np.float32),
        "shf": (-np.random.uniform(0.0, 0.5, (H, 1))).astype(np.float32),
        "unit": (np.random.uniform(0.6, 1.4, (H, 1)) * u[:, None]).astype(np.float32),
        "w3": (n((H, N)) / np.sqrt(H) / u[:, None]).astype(np.float32),
        "offs": striped(np.random.permutation(T)[:S]),
        "bal": striped(np.random.permutation(S)),
    }


def reference(x_words, x_scales, w1, w2, shf, unit, w3, offs, bal):
    xq = unpack_weight(x_words, x_scales)[:, unstriped(offs)]
    yg = mxq(f64(w1), 0, "e4m3").T @ xq
    gate = relu(yg + f64(shf))
    gb = gate[:, unstriped(bal)]
    ld1 = gate.mean(axis=1, keepdims=True)
    gn = gate / (gb + ld1 + 0.5)
    y = mxq(f64(w2), 0, "e4m3").T @ xq
    hid = f64(unit) * (gn * y)
    return mxq(f64(w3), 0, "e4m3").T @ mxq(hid, 0, "e4m3")

@@ -1,0 +1,190 @@
+from contextlib import ExitStack
+
+import concourse.mybir as mybir
+
+K, T, S, N, H = 512, 2048, 512, 256, 512
+FLOPS = 2 * K * H * S * 2 + 2 * H * N * S
+
+F32 = mybir.dt.float32
+BF16 = mybir.dt.bfloat16
+I32 = mybir.dt.int32
+U32 = mybir.dt.uint32
+U16 = mybir.dt.uint16
+U8 = mybir.dt.uint8
+FP8X4 = mybir.dt.float8_e4m3fn_x4
+ACT = mybir.ActivationFunctionType
+ALU = mybir.AluOpType
+
+P = 128
+PACK = 4
+HALF = S // 2
+
+
+def tile_picked_yremoe_norm_p_kernel(
+    tc, x_words, x_scales, w1, w2, shf, unit, w3, offs, bal, out
+):
+    nc = tc.nc
+    with ExitStack() as ctx:
+        sb = ctx.enter_context(tc.tile_pool(name="sb", bufs=1))
+        ps = ctx.enter_context(tc.psum_pool(name="ps", bufs=1))
+
+        offs_sb = sb.tile([P, S // 16], U16, name="offs_sb")
+        bal_sb = sb.tile([P, S // 16], U16, name="bal_sb")
+        words = sb.tile([P, T], U32, name="words")
+        scale_rows = sb.tile([P, T], U8, name="scale_rows")
+        shf_sb = sb.tile([P, PACK], F32, name="shf_sb")
+        unit_sb = sb.tile([P, PACK], F32, name="unit_sb")
+
+        nc.vector.memset(scale_rows[:, : T // 2].bitcast(I32), 0)
+        nc.gpsimd.memset(scale_rows[:, T // 2 :].bitcast(I32), 0)
+        nc.scalar.dma_start(out=shf_sb[:], in_=shf.rearrange("(p t) o -> p (t o)", t=PACK))
+        nc.scalar.dma_start(out=unit_sb[:], in_=unit.rearrange("(p t) o -> p (t o)", t=PACK))
+        for q in range(4):
+            nc.scalar.dma_start(
+                out=scale_rows[32 * q : 32 * q + 4, :].bitcast(I32),
+                in_=x_scales[0, 4 * q : 4 * q + 4, :].bitcast(I32),
+            )
+        nc.sync.dma_start(offs_sb[:], offs)
+        nc.sync.dma_start(bal_sb[:], bal)
+
+        def load_half(w, name, h):
+            rows = w.rearrange("(p j) c -> p j c", j=PACK)
+            raw = sb.tile([P, PACK, H // 2], F32, name=f"{name}_raw{h}")
+            nc.sync.dma_start(out=raw[:], in_=rows[:, :, h * (H // 2) : (h + 1) * (H // 2)])
+            return raw
+
+        w1_raw = [load_half(w1, "w1", 0)]
+        nc.sync.dma_start(
+            out=words[:].bitcast(I32), in_=x_words[0].rearrange("p n r -> p (n r)").bitcast(I32)
+        )
+        w1_raw.append(load_half(w1, "w1", 1))
+        w2_raw = [load_half(w2, "w2", h) for h in range(2)]
+        w3_raw = sb.tile([P, PACK, N], F32, name="w3_raw")
+        nc.sync.dma_start(out=w3_raw[:], in_=w3.rearrange("(p t) m -> p t m", t=PACK))
+
+        table_warm = sb.tile([P, 1], F32, name="table_warm")
+        nc.scalar.activation(table_warm[:], shf_sb[:, 0:1], ACT.Abs_reciprocal_sqrt, bias=1.0, scale=0.0)
+
+        x_codes = sb.tile([P, S], U32, name="x_codes", align_bytes=64)
+        x_bytes = sb.tile([P, S], U8, name="x_bytes", align_bytes=64)
+        nc.vector.tensor_copy(x_bytes[:], scale_rows[:].indirect(offs_sb[:]))
+        nc.vector.tensor_copy(x_codes[:], words[:].indirect(offs_sb[:]))
+
+        def deal_and_quantize(raw_halves, name, copies):
+            planes = []
+            for s in range(2):
+                grouped = sb.tile([P, 2, P, PACK], BF16, name=f"{name}_bf{s}", align_bytes=64)
+                for h in range(2):
+                    copies[s](
+                        out=grouped[:, :, 64 * h : 64 * (h + 1), :].rearrange("p e m j -> p m j e"),
+                        in_=raw_halves[h][:].rearrange("p j (m t) -> p m j t", t=PACK)[:, :, :, 2 * s : 2 * s + 2],
+                    )
+                codes = sb.tile([P, 2 * P], U32, name=f"{name}_codes{s}", align_bytes=64)
+                scales = sb.tile([P, 2 * P], U8, name=f"{name}_scales{s}", align_bytes=64)
+                nc.vector.quantize_mx(
+                    out=codes[:].bitcast(FP8X4),
+                    scales=scales[:],
+                    in_=grouped[:].rearrange("p e m j -> p (e m j)"),
+                )
+                for e in range(2):
+                    planes.append((codes[:, e * P : (e + 1) * P], scales[:, e * P : (e + 1) * P]))
+            return planes
+
+        def project(plane, tag):
+            acc = ps.tile([P, S], F32, name=tag, tag=tag)
+            nc.tensor.matmul_mx(
+                out=acc[:],
+                lhsT=plane[0].bitcast(FP8X4),
+                lhsT_scale=plane[1],
+                rhs=x_codes[:].bitcast(FP8X4),
+                rhs_scale=x_bytes[:],
+                start=True,
+                stop=True,
+            )
+            return acc
+
+        w1_planes = deal_and_quantize(w1_raw, "w1", (nc.vector.tensor_copy, nc.scalar.copy))
+        yg = [project(w1_planes[t], f"bank{t}") for t in range(PACK)]
+
+        row_sum = sb.tile([P, PACK], F32, name="row_sum")
+        row_add = sb.tile([P, PACK], F32, name="row_add")
+        gates, recips = [], []
+        for t in range(PACK):
+            col = slice(t, t + 1)
+            gate = sb.tile([P, S], F32, name=f"gate{t}")
+            root = sb.tile([P, S], F32, name=f"root{t}")
+            recip = sb.tile([P, S], F32, name=f"recip{t}")
+            nc.scalar.activation(gate[:], yg[t][:], ACT.Relu, bias=shf_sb[:, col], accum_out=row_sum[:, col])
+            nc.scalar.activation(row_add[:, col], row_sum[:, col], ACT.Copy, bias=0.5, scale=1.0 / S)
+            nc.scalar.activation(root[:], gate[:], ACT.Abs_reciprocal_sqrt, bias=row_add[:, col])
+            nc.scalar.activation(recip[:], root[:], ACT.Square)
+            gates.append(gate)
+            recips.append(recip)
+
+        w2_planes = deal_and_quantize(w2_raw, "w2", (nc.vector.tensor_copy, nc.vector.tensor_copy))
+        y = [project(w2_planes[t], f"bank{PACK + t}") for t in range(PACK)]
+
+        w3_bf = sb.tile([P, N, PACK], BF16, name="w3_bf", align_bytes=64)
+        w3_codes = sb.tile([P, N], U32, name="w3_codes", align_bytes=64)
+        w3_scales = sb.tile([P, N], U8, name="w3_scales", align_bytes=64)
+        nc.vector.tensor_copy(
+            out=w3_bf[:].rearrange("p (c i) t -> p c t i", i=4),
+            in_=w3_raw[:].rearrange("p t (c i) -> p c t i", i=4),
+        )
+        gated = []
+        for t in range(PACK):
+            product = sb.tile([P, S], F32, name=f"gated{t}")
+            nc.vector.scalar_tensor_tensor(
+                product[:], y[t][:], unit_sb[:, t : t + 1], gates[t][:], ALU.mult, ALU.mult
+            )
+            gated.append(product)
+        nc.vector.quantize_mx(
+            out=w3_codes[:].bitcast(FP8X4),
+            scales=w3_scales[:],
+            in_=w3_bf[:].rearrange("p m t -> p (m t)"),
+        )
+
+        hid = [sb.tile([P, PACK, HALF], F32, name=f"hid{h}") for h in range(2)]
+        for t in range(PACK):
+            for h in range(2):
+                nc.vector.tensor_tensor(
+                    hid[h][:, t, :],
+                    recips[t][:].indirect(bal_sb[:, h * (HALF // 16) : (h + 1) * (HALF // 16)]),
+                    gated[t][:, h * HALF : (h + 1) * HALF],
+                    ALU.mult,
+                )
+
+        hid_bf = []
+        for h, copy in enumerate((nc.scalar.copy, nc.vector.tensor_copy)):
+            grouped = sb.tile([P, HALF, PACK], BF16, name=f"hid_bf{h}", align_bytes=64)
+            copy(
+                out=grouped[:].rearrange("p (c i) t -> p c t i", i=4),
+                in_=hid[h][:].rearrange("p t (c i) -> p c t i", i=4),
+            )
+            hid_bf.append(grouped)
+
+        for h in range(2):
+            codes = sb.tile([P, HALF], U32, name=f"hid_codes{h}", align_bytes=64)
+            scales = sb.tile([P, HALF], U8, name=f"hid_scales{h}", align_bytes=64)
+            nc.vector.quantize_mx(
+                out=codes[:].bitcast(FP8X4),
+                scales=scales[:],
+                in_=hid_bf[h][:].rearrange("p n t -> p (n t)"),
+            )
+            for m, (copy, queue) in enumerate(
+                ((nc.scalar.copy, nc.scalar), (nc.vector.tensor_copy, nc.sync))
+            ):
+                tag = f"bank{2 * h + m}"
+                acc = ps.tile([P, HALF], F32, name=tag, tag=tag)
+                nc.tensor.matmul_mx(
+                    out=acc[:],
+                    lhsT=w3_codes[:, m * P : (m + 1) * P].bitcast(FP8X4),
+                    lhsT_scale=w3_scales[:, m * P : (m + 1) * P],
+                    rhs=codes[:].bitcast(FP8X4),
+                    rhs_scale=scales[:],
+                    start=True,
+                    stop=True,
+                )
+                result = sb.tile([P, HALF], F32, name=f"result{h}{m}")
+                copy(out=result[:], in_=acc[:])
+                queue.dma_start(out=out[m * P : (m + 1) * P, h * HALF : (h + 1) * HALF], in_=result[:])

@@ -18,6 +18,9 @@ ALU = mybir.AluOpType
 P = 128
 PACK = 4
 HALF = S // 2
+CHUNK = 128
+CHUNKS = S // CHUNK
+SPARE = 32
 
 
 def tile_picked_yremoe_norm_p_kernel(
@@ -34,51 +37,42 @@ def tile_picked_yremoe_norm_p_kernel(
         scale_rows = sb.tile([P, T], U8, name="scale_rows")
         shf_sb = sb.tile([P, PACK], F32, name="shf_sb")
         unit_sb = sb.tile([P, PACK], F32, name="unit_sb")
+        w1_raw = sb.tile([P, PACK, H], F32, name="w1_raw")
+        w2_raw = sb.tile([P, PACK, H], F32, name="w2_raw")
+        w3_raw = sb.tile([P, PACK, N], F32, name="w3_raw")
 
         nc.vector.memset(scale_rows[:, : T // 2].bitcast(I32), 0)
         nc.gpsimd.memset(scale_rows[:, T // 2 :].bitcast(I32), 0)
-        nc.scalar.dma_start(out=shf_sb[:], in_=shf.rearrange("(p t) o -> p (t o)", t=PACK))
-        nc.scalar.dma_start(out=unit_sb[:], in_=unit.rearrange("(p t) o -> p (t o)", t=PACK))
-        for q in range(4):
-            nc.scalar.dma_start(
-                out=scale_rows[32 * q : 32 * q + 4, :].bitcast(I32),
-                in_=x_scales[0, 4 * q : 4 * q + 4, :].bitcast(I32),
-            )
         nc.sync.dma_start(offs_sb[:], offs)
-        nc.sync.dma_start(bal_sb[:], bal)
-
-        def load_half(w, name, h):
-            rows = w.rearrange("(p j) c -> p j c", j=PACK)
-            raw = sb.tile([P, PACK, H // 2], F32, name=f"{name}_raw{h}")
-            nc.sync.dma_start(out=raw[:], in_=rows[:, :, h * (H // 2) : (h + 1) * (H // 2)])
-            return raw
-
-        w1_raw = [load_half(w1, "w1", 0)]
+        nc.sync.dma_start(out=w1_raw[:], in_=w1.rearrange("(p j) c -> p j c", j=PACK))
+        for r in range(4):
+            nc.sync.dma_start(
+                out=scale_rows[r:P:32, :].bitcast(I32), in_=x_scales[0, r:16:4, :].bitcast(I32)
+            )
         nc.sync.dma_start(
             out=words[:].bitcast(I32), in_=x_words[0].rearrange("p n r -> p (n r)").bitcast(I32)
         )
-        w1_raw.append(load_half(w1, "w1", 1))
-        w2_raw = [load_half(w2, "w2", h) for h in range(2)]
-        w3_raw = sb.tile([P, PACK, N], F32, name="w3_raw")
+        nc.scalar.dma_start(out=shf_sb[:], in_=shf.rearrange("(p t) o -> p (t o)", t=PACK))
+        nc.sync.dma_start(out=w2_raw[:], in_=w2.rearrange("(p j) c -> p j c", j=PACK))
+        nc.scalar.dma_start(out=unit_sb[:], in_=unit.rearrange("(p t) o -> p (t o)", t=PACK))
         nc.sync.dma_start(out=w3_raw[:], in_=w3.rearrange("(p t) m -> p t m", t=PACK))
+        nc.sync.dma_start(bal_sb[:], bal)
 
         table_warm = sb.tile([P, 1], F32, name="table_warm")
-        nc.scalar.activation(table_warm[:], shf_sb[:, 0:1], ACT.Abs_reciprocal_sqrt, bias=1.0, scale=0.0)
+        nc.scalar.activation(table_warm[:], w1_raw[:, 0, 0:1], ACT.Abs_reciprocal_sqrt, bias=1.0, scale=0.0)
 
-        x_codes = sb.tile([P, S], U32, name="x_codes", align_bytes=64)
-        x_bytes = sb.tile([P, S], U8, name="x_bytes", align_bytes=64)
-        nc.vector.tensor_copy(x_bytes[:], scale_rows[:].indirect(offs_sb[:]))
-        nc.vector.tensor_copy(x_codes[:], words[:].indirect(offs_sb[:]))
+        recips = [sb.tile([P, S + SPARE if t < 2 else S], F32, name=f"recip{t}") for t in range(PACK)]
+        for recip in recips[:2]:
+            nc.gpsimd.memset(recip[:, S:], 0.0)
 
-        def deal_and_quantize(raw_halves, name, copies):
+        def deal_and_quantize(raw, name, copies):
             planes = []
             for s in range(2):
-                grouped = sb.tile([P, 2, P, PACK], BF16, name=f"{name}_bf{s}", align_bytes=64)
-                for h in range(2):
-                    copies[s](
-                        out=grouped[:, :, 64 * h : 64 * (h + 1), :].rearrange("p e m j -> p m j e"),
-                        in_=raw_halves[h][:].rearrange("p j (m t) -> p m j t", t=PACK)[:, :, :, 2 * s : 2 * s + 2],
-                    )
+                grouped = sb.tile([P, 2, P, PACK], BF16, name=f"{name}_bf{s}", tag=f"{name}_bf{s}", align_bytes=64)
+                copies[s](
+                    out=grouped[:].rearrange("p e m j -> p m j e"),
+                    in_=raw[:].rearrange("p j (m t) -> p m j t", t=PACK)[:, :, :, 2 * s : 2 * s + 2],
+                )
                 codes = sb.tile([P, 2 * P], U32, name=f"{name}_codes{s}", align_bytes=64)
                 scales = sb.tile([P, 2 * P], U8, name=f"{name}_scales{s}", align_bytes=64)
                 nc.vector.quantize_mx(
@@ -90,47 +84,65 @@ def tile_picked_yremoe_norm_p_kernel(
                     planes.append((codes[:, e * P : (e + 1) * P], scales[:, e * P : (e + 1) * P]))
             return planes
 
-        def project(plane, tag):
-            acc = ps.tile([P, S], F32, name=tag, tag=tag)
-            nc.tensor.matmul_mx(
-                out=acc[:],
-                lhsT=plane[0].bitcast(FP8X4),
-                lhsT_scale=plane[1],
-                rhs=x_codes[:].bitcast(FP8X4),
-                rhs_scale=x_bytes[:],
-                start=True,
-                stop=True,
+        w1_planes = deal_and_quantize(w1_raw, "w1", (nc.vector.tensor_copy, nc.scalar.copy))
+
+        x_codes = sb.tile([P, S], U32, name="x_codes", align_bytes=64)
+        x_bytes = sb.tile([P, S], U8, name="x_bytes", align_bytes=64)
+        nc.vector.tensor_copy(x_bytes[:], scale_rows[:].indirect(offs_sb[:]))
+        for h in range(2):
+            nc.vector.tensor_copy(
+                x_codes[:, h * HALF : (h + 1) * HALF],
+                words[:].indirect(offs_sb[:, h * (HALF // 16) : (h + 1) * (HALF // 16)]),
             )
+
+        def project(plane, tag, width):
+            acc = ps.tile([P, S], F32, name=tag, tag=tag)
+            for c in range(0, S, width):
+                nc.tensor.matmul_mx(
+                    out=acc[:, c : c + width],
+                    lhsT=plane[0].bitcast(FP8X4),
+                    lhsT_scale=plane[1],
+                    rhs=x_codes[:, c : c + width].bitcast(FP8X4),
+                    rhs_scale=x_bytes[:, c : c + width],
+                    start=True,
+                    stop=True,
+                )
             return acc
 
-        w1_planes = deal_and_quantize(w1_raw, "w1", (nc.vector.tensor_copy, nc.scalar.copy))
-        yg = [project(w1_planes[t], f"bank{t}") for t in range(PACK)]
+        yg = [project(w1_planes[t], f"bank{t}", HALF) for t in range(PACK)]
 
         row_sum = sb.tile([P, PACK], F32, name="row_sum")
         row_add = sb.tile([P, PACK], F32, name="row_add")
-        gates, recips = [], []
+        gates = []
+        roots = []
         for t in range(PACK):
-            col = slice(t, t + 1)
             gate = sb.tile([P, S], F32, name=f"gate{t}")
-            root = sb.tile([P, S], F32, name=f"root{t}")
-            recip = sb.tile([P, S], F32, name=f"recip{t}")
-            nc.scalar.activation(gate[:], yg[t][:], ACT.Relu, bias=shf_sb[:, col], accum_out=row_sum[:, col])
-            nc.scalar.activation(row_add[:, col], row_sum[:, col], ACT.Copy, bias=0.5, scale=1.0 / S)
-            nc.scalar.activation(root[:], gate[:], ACT.Abs_reciprocal_sqrt, bias=row_add[:, col])
-            nc.scalar.activation(recip[:], root[:], ACT.Square)
+            nc.scalar.activation(
+                gate[:], yg[t][:], ACT.Relu, bias=shf_sb[:, t : t + 1], accum_out=row_sum[:, t : t + 1]
+            )
             gates.append(gate)
-            recips.append(recip)
+            if t % 2 == 1:
+                pair = slice(t - 1, t + 1)
+                nc.scalar.activation(row_add[:, pair], row_sum[:, pair], ACT.Copy, bias=0.5, scale=1.0 / S)
+        for t in range(PACK):
+            root = sb.tile([P, S], F32, name=f"root{t}")
+            nc.scalar.activation(root[:], gates[t][:], ACT.Abs_reciprocal_sqrt, bias=row_add[:, t : t + 1])
+            nc.scalar.activation(recips[t][:, :S], root[:], ACT.Square)
 
         w2_planes = deal_and_quantize(w2_raw, "w2", (nc.vector.tensor_copy, nc.vector.tensor_copy))
-        y = [project(w2_planes[t], f"bank{PACK + t}") for t in range(PACK)]
+        y = [project(w2_planes[t], f"bank{PACK + t}", S) for t in range(PACK)]
 
-        w3_bf = sb.tile([P, N, PACK], BF16, name="w3_bf", align_bytes=64)
+        w3_bf = sb.tile([P, N, PACK], BF16, name="w3_bf", tag="w2_bf1", align_bytes=64)
+        nc.gpsimd.tensor_scalar(
+            w3_bf[:].rearrange("p (c i) t -> p c t i", i=4),
+            w3_raw[:].rearrange("p t (c i) -> p c t i", i=4),
+            1.0,
+            0.0,
+            ALU.mult,
+            ALU.add,
+        )
         w3_codes = sb.tile([P, N], U32, name="w3_codes", align_bytes=64)
         w3_scales = sb.tile([P, N], U8, name="w3_scales", align_bytes=64)
-        nc.vector.tensor_copy(
-            out=w3_bf[:].rearrange("p (c i) t -> p c t i", i=4),
-            in_=w3_raw[:].rearrange("p t (c i) -> p c t i", i=4),
-        )
         gated = []
         for t in range(PACK):
             product = sb.tile([P, S], F32, name=f"gated{t}")
@@ -138,46 +150,49 @@ def tile_picked_yremoe_norm_p_kernel(
                 product[:], y[t][:], unit_sb[:, t : t + 1], gates[t][:], ALU.mult, ALU.mult
             )
             gated.append(product)
+
+        hid = sb.tile([P, PACK, S], F32, name="hid")
+        def look_up(t, start, width):
+            nc.vector.tensor_tensor(
+                hid[:, t, start : start + width],
+                recips[t][:].indirect(bal_sb[:, start // 16 : (start + width) // 16]),
+                gated[t][:, start : start + width],
+                ALU.mult,
+            )
+
+        look_up(0, 0, S)
+        look_up(1, 0, S)
         nc.vector.quantize_mx(
             out=w3_codes[:].bitcast(FP8X4),
             scales=w3_scales[:],
             in_=w3_bf[:].rearrange("p m t -> p (m t)"),
         )
-
-        hid = [sb.tile([P, PACK, HALF], F32, name=f"hid{h}") for h in range(2)]
-        for t in range(PACK):
-            for h in range(2):
-                nc.vector.tensor_tensor(
-                    hid[h][:, t, :],
-                    recips[t][:].indirect(bal_sb[:, h * (HALF // 16) : (h + 1) * (HALF // 16)]),
-                    gated[t][:, h * HALF : (h + 1) * HALF],
-                    ALU.mult,
-                )
+        for start in range(0, S, CHUNK):
+            look_up(2, start, CHUNK)
+            look_up(3, start, CHUNK)
 
         hid_bf = []
-        for h, copy in enumerate((nc.scalar.copy, nc.vector.tensor_copy)):
-            grouped = sb.tile([P, HALF, PACK], BF16, name=f"hid_bf{h}", align_bytes=64)
+        for c in range(CHUNKS):
+            copy = nc.scalar.copy
+            grouped = sb.tile([P, CHUNK, PACK], BF16, name=f"hid_bf{c}", align_bytes=64)
             copy(
-                out=grouped[:].rearrange("p (c i) t -> p c t i", i=4),
-                in_=hid[h][:].rearrange("p t (c i) -> p c t i", i=4),
+                out=grouped[:].rearrange("p (g i) t -> p g t i", i=4),
+                in_=hid[:, :, c * CHUNK : (c + 1) * CHUNK].rearrange("p t (g i) -> p g t i", i=4),
             )
             hid_bf.append(grouped)
 
-        for h in range(2):
-            codes = sb.tile([P, HALF], U32, name=f"hid_codes{h}", align_bytes=64)
-            scales = sb.tile([P, HALF], U8, name=f"hid_scales{h}", align_bytes=64)
+        for c in range(CHUNKS):
+            codes = sb.tile([P, CHUNK], U32, name=f"hid_codes{c}", align_bytes=64)
+            scales = sb.tile([P, CHUNK], U8, name=f"hid_scales{c}", align_bytes=64)
             nc.vector.quantize_mx(
                 out=codes[:].bitcast(FP8X4),
                 scales=scales[:],
-                in_=hid_bf[h][:].rearrange("p n t -> p (n t)"),
+                in_=hid_bf[c][:].rearrange("p n t -> p (n t)"),
             )
-            for m, (copy, queue) in enumerate(
-                ((nc.scalar.copy, nc.scalar), (nc.vector.tensor_copy, nc.sync))
-            ):
-                tag = f"bank{2 * h + m}"
-                acc = ps.tile([P, HALF], F32, name=tag, tag=tag)
+            acc = ps.tile([P, 2, CHUNK], F32, name=f"bank{c}", tag=f"bank{c}")
+            for m in range(2):
                 nc.tensor.matmul_mx(
-                    out=acc[:],
+                    out=acc[:, m, :],
                     lhsT=w3_codes[:, m * P : (m + 1) * P].bitcast(FP8X4),
                     lhsT_scale=w3_scales[:, m * P : (m + 1) * P],
                     rhs=codes[:].bitcast(FP8X4),
@@ -185,6 +200,9 @@ def tile_picked_yremoe_norm_p_kernel(
                     start=True,
                     stop=True,
                 )
-                result = sb.tile([P, HALF], F32, name=f"result{h}{m}")
-                copy(out=result[:], in_=acc[:])
-                queue.dma_start(out=out[m * P : (m + 1) * P, h * HALF : (h + 1) * HALF], in_=result[:])
+            result = sb.tile([P, 2, CHUNK], F32, name=f"result{c}")
+            copy, queue = (nc.vector.tensor_copy if c == 2 else nc.scalar.copy), nc.sync
+            copy(out=result[:], in_=acc[:])
+            queue.dma_start(
+                out=out.rearrange("(m p) n -> p m n", p=P)[:, :, c * CHUNK : (c + 1) * CHUNK], in_=result[:]
+            )

from contextlib import ExitStack

import concourse.mybir as mybir

K, T, S, N, H = 512, 2048, 512, 256, 512
FLOPS = 2 * K * H * S * 2 + 2 * H * N * S

F32 = mybir.dt.float32
BF16 = mybir.dt.bfloat16
I32 = mybir.dt.int32
U32 = mybir.dt.uint32
U16 = mybir.dt.uint16
U8 = mybir.dt.uint8
FP8X4 = mybir.dt.float8_e4m3fn_x4
ACT = mybir.ActivationFunctionType
ALU = mybir.AluOpType

P = 128
PACK = 4
HALF = S // 2
CHUNK = 128
CHUNKS = S // CHUNK
SPARE = 32


def tile_picked_yremoe_norm_p_kernel(
    tc, x_words, x_scales, w1, w2, shf, unit, w3, offs, bal, out
):
    nc = tc.nc
    with ExitStack() as ctx:
        sb = ctx.enter_context(tc.tile_pool(name="sb", bufs=1))
        ps = ctx.enter_context(tc.psum_pool(name="ps", bufs=1))

        offs_sb = sb.tile([P, S // 16], U16, name="offs_sb")
        bal_sb = sb.tile([P, S // 16], U16, name="bal_sb")
        words = sb.tile([P, T], U32, name="words")
        scale_rows = sb.tile([P, T], U8, name="scale_rows")
        shf_sb = sb.tile([P, PACK], F32, name="shf_sb")
        unit_sb = sb.tile([P, PACK], F32, name="unit_sb")
        w1_raw = sb.tile([P, PACK, H], F32, name="w1_raw")
        w2_raw = sb.tile([P, PACK, H], F32, name="w2_raw")
        w3_raw = sb.tile([P, PACK, N], F32, name="w3_raw")

        nc.vector.memset(scale_rows[:, : T // 2].bitcast(I32), 0)
        nc.gpsimd.memset(scale_rows[:, T // 2 :].bitcast(I32), 0)
        nc.sync.dma_start(offs_sb[:], offs)
        nc.sync.dma_start(out=w1_raw[:], in_=w1.rearrange("(p j) c -> p j c", j=PACK))
        for r in range(4):
            nc.sync.dma_start(
                out=scale_rows[r:P:32, :].bitcast(I32), in_=x_scales[0, r:16:4, :].bitcast(I32)
            )
        nc.sync.dma_start(
            out=words[:].bitcast(I32), in_=x_words[0].rearrange("p n r -> p (n r)").bitcast(I32)
        )
        nc.scalar.dma_start(out=shf_sb[:], in_=shf.rearrange("(p t) o -> p (t o)", t=PACK))
        nc.sync.dma_start(out=w2_raw[:], in_=w2.rearrange("(p j) c -> p j c", j=PACK))
        nc.scalar.dma_start(out=unit_sb[:], in_=unit.rearrange("(p t) o -> p (t o)", t=PACK))
        nc.sync.dma_start(out=w3_raw[:], in_=w3.rearrange("(p t) m -> p t m", t=PACK))
        nc.sync.dma_start(bal_sb[:], bal)

        table_warm = sb.tile([P, 1], F32, name="table_warm")
        nc.scalar.activation(table_warm[:], w1_raw[:, 0, 0:1], ACT.Abs_reciprocal_sqrt, bias=1.0, scale=0.0)

        recips = [sb.tile([P, S + SPARE if t < 2 else S], F32, name=f"recip{t}") for t in range(PACK)]
        for recip in recips[:2]:
            nc.gpsimd.memset(recip[:, S:], 0.0)

        def deal_and_quantize(raw, name, copies):
            planes = []
            for s in range(2):
                grouped = sb.tile([P, 2, P, PACK], BF16, name=f"{name}_bf{s}", tag=f"{name}_bf{s}", align_bytes=64)
                copies[s](
                    out=grouped[:].rearrange("p e m j -> p m j e"),
                    in_=raw[:].rearrange("p j (m t) -> p m j t", t=PACK)[:, :, :, 2 * s : 2 * s + 2],
                )
                codes = sb.tile([P, 2 * P], U32, name=f"{name}_codes{s}", align_bytes=64)
                scales = sb.tile([P, 2 * P], U8, name=f"{name}_scales{s}", align_bytes=64)
                nc.vector.quantize_mx(
                    out=codes[:].bitcast(FP8X4),
                    scales=scales[:],
                    in_=grouped[:].rearrange("p e m j -> p (e m j)"),
                )
                for e in range(2):
                    planes.append((codes[:, e * P : (e + 1) * P], scales[:, e * P : (e + 1) * P]))
            return planes

        w1_planes = deal_and_quantize(w1_raw, "w1", (nc.vector.tensor_copy, nc.scalar.copy))

        x_codes = sb.tile([P, S], U32, name="x_codes", align_bytes=64)
        x_bytes = sb.tile([P, S], U8, name="x_bytes", align_bytes=64)
        nc.vector.tensor_copy(x_bytes[:], scale_rows[:].indirect(offs_sb[:]))
        for h in range(2):
            nc.vector.tensor_copy(
                x_codes[:, h * HALF : (h + 1) * HALF],
                words[:].indirect(offs_sb[:, h * (HALF // 16) : (h + 1) * (HALF // 16)]),
            )

        def project(plane, tag, width):
            acc = ps.tile([P, S], F32, name=tag, tag=tag)
            for c in range(0, S, width):
                nc.tensor.matmul_mx(
                    out=acc[:, c : c + width],
                    lhsT=plane[0].bitcast(FP8X4),
                    lhsT_scale=plane[1],
                    rhs=x_codes[:, c : c + width].bitcast(FP8X4),
                    rhs_scale=x_bytes[:, c : c + width],
                    start=True,
                    stop=True,
                )
            return acc

        yg = [project(w1_planes[t], f"bank{t}", HALF) for t in range(PACK)]

        row_sum = sb.tile([P, PACK], F32, name="row_sum")
        row_add = sb.tile([P, PACK], F32, name="row_add")
        gates = []
        roots = []
        for t in range(PACK):
            gate = sb.tile([P, S], F32, name=f"gate{t}")
            nc.scalar.activation(
                gate[:], yg[t][:], ACT.Relu, bias=shf_sb[:, t : t + 1], accum_out=row_sum[:, t : t + 1]
            )
            gates.append(gate)
            if t % 2 == 1:
                pair = slice(t - 1, t + 1)
                nc.scalar.activation(row_add[:, pair], row_sum[:, pair], ACT.Copy, bias=0.5, scale=1.0 / S)
        for t in range(PACK):
            root = sb.tile([P, S], F32, name=f"root{t}")
            nc.scalar.activation(root[:], gates[t][:], ACT.Abs_reciprocal_sqrt, bias=row_add[:, t : t + 1])
            nc.scalar.activation(recips[t][:, :S], root[:], ACT.Square)

        w2_planes = deal_and_quantize(w2_raw, "w2", (nc.vector.tensor_copy, nc.vector.tensor_copy))
        y = [project(w2_planes[t], f"bank{PACK + t}", S) for t in range(PACK)]

        w3_bf = sb.tile([P, N, PACK], BF16, name="w3_bf", tag="w2_bf1", align_bytes=64)
        nc.gpsimd.tensor_scalar(
            w3_bf[:].rearrange("p (c i) t -> p c t i", i=4),
            w3_raw[:].rearrange("p t (c i) -> p c t i", i=4),
            1.0,
            0.0,
            ALU.mult,
            ALU.add,
        )
        w3_codes = sb.tile([P, N], U32, name="w3_codes", align_bytes=64)
        w3_scales = sb.tile([P, N], U8, name="w3_scales", align_bytes=64)
        gated = []
        for t in range(PACK):
            product = sb.tile([P, S], F32, name=f"gated{t}")
            nc.vector.scalar_tensor_tensor(
                product[:], y[t][:], unit_sb[:, t : t + 1], gates[t][:], ALU.mult, ALU.mult
            )
            gated.append(product)

        hid = sb.tile([P, PACK, S], F32, name="hid")
        def look_up(t, start, width):
            nc.vector.tensor_tensor(
                hid[:, t, start : start + width],
                recips[t][:].indirect(bal_sb[:, start // 16 : (start + width) // 16]),
                gated[t][:, start : start + width],
                ALU.mult,
            )

        look_up(0, 0, S)
        look_up(1, 0, S)
        nc.vector.quantize_mx(
            out=w3_codes[:].bitcast(FP8X4),
            scales=w3_scales[:],
            in_=w3_bf[:].rearrange("p m t -> p (m t)"),
        )
        for start in range(0, S, CHUNK):
            look_up(2, start, CHUNK)
            look_up(3, start, CHUNK)

        hid_bf = []
        for c in range(CHUNKS):
            copy = nc.scalar.copy
            grouped = sb.tile([P, CHUNK, PACK], BF16, name=f"hid_bf{c}", align_bytes=64)
            copy(
                out=grouped[:].rearrange("p (g i) t -> p g t i", i=4),
                in_=hid[:, :, c * CHUNK : (c + 1) * CHUNK].rearrange("p t (g i) -> p g t i", i=4),
            )
            hid_bf.append(grouped)

        for c in range(CHUNKS):
            codes = sb.tile([P, CHUNK], U32, name=f"hid_codes{c}", align_bytes=64)
            scales = sb.tile([P, CHUNK], U8, name=f"hid_scales{c}", align_bytes=64)
            nc.vector.quantize_mx(
                out=codes[:].bitcast(FP8X4),
                scales=scales[:],
                in_=hid_bf[c][:].rearrange("p n t -> p (n t)"),
            )
            acc = ps.tile([P, 2, CHUNK], F32, name=f"bank{c}", tag=f"bank{c}")
            for m in range(2):
                nc.tensor.matmul_mx(
                    out=acc[:, m, :],
                    lhsT=w3_codes[:, m * P : (m + 1) * P].bitcast(FP8X4),
                    lhsT_scale=w3_scales[:, m * P : (m + 1) * P],
                    rhs=codes[:].bitcast(FP8X4),
                    rhs_scale=scales[:],
                    start=True,
                    stop=True,
                )
            result = sb.tile([P, 2, CHUNK], F32, name=f"result{c}")
            copy, queue = (nc.vector.tensor_copy if c == 2 else nc.scalar.copy), nc.sync
            copy(out=result[:], in_=acc[:])
            queue.dma_start(
                out=out.rearrange("(m p) n -> p m n", p=P)[:, :, c * CHUNK : (c + 1) * CHUNK], in_=result[:]
            )
